import numpy as np, ml_dtypes
CORES = [48,51,52,55]
N = 4
import mx_ref
BF = ml_dtypes.bfloat16
def gcols(t, e):
    v = np.concatenate([t.reshape(8, 16, -1, 4), np.zeros((8, 16, 1, 4), BF)], axis=2)
    return np.ascontiguousarray(np.stack([v[g][:, e[g]] for g in range(8)])).reshape(128, -1)
def tile(rs):
    return np.stack(rs, axis=2).reshape(128, -1).astype(BF)
def pick(q, e):
    c = np.concatenate([q[0].reshape(128, -1, 4), np.zeros((128, 1, 4), np.uint8)], axis=1); s = np.concatenate([q[1], np.ones((16, 1), np.uint8)], axis=1)
    return (np.ascontiguousarray(c[:, e].reshape(128, -1)), np.ascontiguousarray(s[:, e]))
def join(*qs):
    return (np.concatenate([q[0] for q in qs], axis=1), np.concatenate([q[1] for q in qs], axis=1))
def put(q, e, v):
    c, s = q[0].reshape(128, -1, 4).copy(), q[1].copy(); c[:, e] = v[0].reshape(128, -1, 4); s[:, e] = v[1]
    return (c.reshape(128, -1), s)
def pk(c, s):
    return (np.ascontiguousarray(c), mx_ref.live(s))
def emit(q):
    return q[0], q[1]
def packed(v, rng):
    q = [mx_ref.quantize(np.ascontiguousarray(v[r])) for r in range(N)]
    return np.stack([a for a, b in q]), np.stack([mx_ref.plane(b, rng) for a, b in q])
def values_of_codes():
    e, c = np.zeros((128, 128, 4), np.float32), np.zeros((128, 2, 4), np.uint8)
    e[np.arange(128), np.arange(128), 0] = 1
    c[:127, :, 0] = np.arange(256).reshape(2, 128).T[:127]
    return mx_ref.matmul(mx_ref.quantize(e.reshape(128, 512).astype(BF)), (c.reshape(128, 8), np.full((16, 2), 127, np.uint8))).T.reshape(-1).astype(np.float64)
CODE_VALUE, SCALE_VALUE = values_of_codes(), 2.0 ** (np.arange(256) - 127.0)
def decode(q):
    return (CODE_VALUE[q[0]].reshape(16, 8, -1, 4) * SCALE_VALUE[q[1]][:, None, :, None] + 0.0).reshape(128, -1).astype(np.float32)
def f(rng, *shape):
    return mx_ref.flush((rng.standard_normal(shape, dtype=np.float32) * np.exp2(rng.integers(-2, 3, shape[:-1] + (1,)))).astype(BF))
def wide(rng, *shape, cols=0):
    v = rng.standard_normal(shape, dtype=np.float32) * np.exp2(rng.integers(-12, 13, shape)).astype(np.float32)
    if cols: v *= np.repeat(np.exp2(rng.integers(-cols, cols + 1, shape[:-2] + (1, shape[-1] // 4))) * (rng.random(shape[:-2] + (1, shape[-1] // 4)) > 0.0625), 4, axis=-1).astype(np.float32)
    return mx_ref.flush(v.astype(BF))
C, A, STEP = 256, 12, [2, 1]
def big(v):
    v = v.astype(np.float32)
    v[np.abs(v) < np.float32(2.0 ** -16)] = 0
    return v.astype(BF)
def numbers_of(rng):
    return {"x": big(f(rng, N, 128, 4 * C)), "u": np.array(f(rng, N, 128, 512)), "v": np.array(f(rng, N, 128, 512))}
def layers(rng):
    return big(rng.random((N, 128, 2048), dtype=np.float32) * 2 - 1).reshape(N, 8, 16, 4, 8, 16, 4)
def weights(rng, w):
    c, s = packed(np.ascontiguousarray(w).reshape(N, 128, 2048), rng)
    return {"wc": c, "ws": s}
def setup_inputs(rng):
    return {**numbers_of(rng), **weights(rng, layers(rng))}
def setup_inputs_ties(rng):
    d = numbers_of(rng)
    o = rng.permutation(N)
    x = d["x"].reshape(N, 8, 16, C, 4)
    x[:, :, :8] = 0
    x[:, :, 0, :, 0] = rng.integers(0, 4, (N, 8, C)).astype(np.float32).astype(BF)
    t = rng.integers(-1, 2, (N, 8, C, 3))
    t[o[0]] = -1
    t[o[0], :, A::A + 1, 0] = 1
    t[o[1]] = 1
    x[:, :, 1, :, :3] = t.astype(np.float32).astype(BF)
    u = d["u"].reshape(N, 128, 128, 4)
    for i in range(4): u[:, :, i::16] = 0
    for r in range(N):
        for h in range(0, 128, 16):
            u[r, h, h, 0] = 0.0 if r == o[0] else -1.0 if r == o[2] else 1.0
            for i in range(3): u[r, h + 1, h + 1 + i, i] = 1.0
    w = layers(rng)
    w[:, :, :, :, :, :8] = 0
    return {"x": x.reshape(N, 128, 4 * C), "u": u.reshape(N, 128, 512), "v": d["v"], **weights(rng, w)}
def setup_inputs_near(rng):
    d = numbers_of(rng)
    x = d["x"].astype(np.float32).reshape(N, 8, 16, C, 4)
    x[:, :, 0] = 0
    x[:, :, 8:] = 0
    u = d["u"].reshape(N, 128, 128, 4)
    for i in range(4): u[:, :, i::16] = 0
    o = rng.permutation(N) % 4
    for r in range(N):
        tiny = o[r] == 2
        k = 2.0 ** -30 if o[r] == 1 else 1.0
        if tiny:
            m = rng.integers(0, 8, (8, C))
            x[r, :, 8, :, 0] = (8 + m) * 2.0 ** -33
            x[r, :, 9, :, 0] = (15 - m) * 2.0 ** -33
        else:
            s = rng.integers(0, 16, (8, C))
            x[r, :, 0, :, 0] = 1.0 if o[r] == 0 else -1.0 if o[r] == 1 else rng.choice([-1.0, 1.0], (8, C))
            x[r, :, 8] = ((s[:, :, None] >> np.arange(4)) & 1) * np.exp2(np.arange(4) - 23.0)
            x[r, :, 11, :, 0] = 2.0 ** -10
        x[r, :, 12:15, :, 0] = rng.integers(-1, 2, (8, 3, C)) * (2.0 ** -30 if tiny else 2.0 ** -22)
        if o[r] in (0, 2):
            for g in rng.permutation(8)[:4]: x[r, g, 0, rng.integers(C), 1] = rng.choice([-1.0, 1.0]) * 2.0 ** 21
        for h in range(0, 128, 16):
            if tiny:
                u[r, h + 8, h, 0] = 1.125 * 2.0 ** -30
                u[r, h + 9, h, 0] = 2.0 ** -30
            else:
                u[r, h, h, 0] = k
                u[r, h + 8, h] = k
                u[r, h + 11, h, 0] = k
            if o[r] in (0, 2): u[r, h, h, 1] = 2.0 ** 9
            for i in range(3): u[r, h + 12 + i, h + 1 + i, 0] = 2.0 ** -30
    w = layers(rng)
    for i in [0, 8, 9, 10, 11, 12, 13, 14, 15]:
        w[:, :, i] = 0
        w[:, :, :, :, :, i] = 0
    return {"x": x.reshape(N, 128, 4 * C).astype(BF), "u": u.reshape(N, 128, 512), "v": d["v"], **weights(rng, w)}
def setup_inputs_ends(rng):
    d = numbers_of(rng)
    e = rng.permutation(N)
    top = e[0] ^ STEP[0] ^ STEP[1]
    mate = top ^ STEP[0]
    rest = [r for r in e[1:] if r not in (top, mate)]
    e = [e[0]] + rest[:N // 2 - 1] + [top, mate] + rest[N // 2 - 1:]
    c = rng.integers(8)
    x = np.zeros((N, 8, 16, C, 4), np.float32)
    u = d["u"].astype(np.float32).reshape(N, 8, 16, 128, 4)
    for i in range(4): u[:, :, :, i::16] = 0
    v = rng.choice([-1.0, 1.0], (N, 128, 512)).astype(np.float32)
    sign = lambda *s: rng.choice([-1.0, 1.0], s)
    for r in range(N):
        h = rng.permutation(8)
        if r in e[:N // 2]:
            t = sign(4, 1, 1, 1)
            if r == e[0]: t[:] = -1
            m = sign(8, 1, C, 1) * rng.choice([0.5, 0.75, 0.875, 1.0], (8, 1, C, 1))
            m[h[4:, None], 0, rng.permutation(C)[:64], 0] = -rng.choice([0.75, 0.875, 1.0], (4, 64))
            p = (m[h[4:]] > 0).all(axis=0)
            m[h[4]][p] *= -1
            m[h[:4]] = t
            x[r] = 2.0 ** 21 * m
            v[r] *= np.float32(2.0 ** 30)
            for n in range(8):
                g = h[n]
                if n < 4: u[r, h[:4], :, 16 * g] = -2.0 ** 30 * t[:, :, 0]
                if n in (2, 3): u[r, h[4:], :, 16 * g] = 2.0 ** 29 if n == 2 else 2.0 ** 30
                if n >= 4: u[r, h[4:], :, 16 * g] = 2.0 ** 30 * sign(4, 1, 1)
                for i in range(3): u[r, rng.choice(h[4:]), :, 16 * g + 1 + i] = 2.0 ** 30 * rng.choice([-1.0, 1.0])
        elif r == top:
            x[r] = 2.0 ** 21
            s = (rng.permutation(C)[:, None] >> np.arange(8)) & 1
            x[r, c, :2] = 2.0 ** 21 * (2.0 * s - 1.0).reshape(C, 2, 4).transpose(1, 0, 2)
            v[r] *= np.float32(2.0 ** 30)
            for n in range(8):
                g = h[n]
                u[r, :, :, 16 * g] = -2.0 ** 30 if n < 4 else 2.0 ** 30
                k = 4.0 * rng.permutation(2)[:, None] + rng.permutation(4)
                u[r, c, :2, 16 * g] *= np.exp2(-k).astype(np.float32)
        else:
            x[r, :, :8] = 2.0 ** -30 * sign(8, 1, C, 1)
            x[r, :, 8:] = sign(8, 1, C, 1)
            v[r] *= np.float32(2.0 ** -30)
            for n in range(8):
                g = h[n]
                if n >= 2: u[r, :, :8, 16 * g] = 2.0 ** -30 * sign(8, 1, 1)
                for i in range(3): u[r, rng.integers(8), :8, 16 * g + 1 + i] = 2.0 ** -30 * rng.choice([-1.0, 1.0])
    w = rng.choice([-1.0, 1.0], (N, 8, 16, 4, 8, 16, 4)).astype(np.float32)
    w[e[0]] = 1
    w[e[1]] = 0
    w[:, :, :8] = 0
    w[:, :, :, :, :, :8] = 0
    w[mate] = 1
    w[mate, c, :2] = 0
    return {"x": x.reshape(N, 128, 4 * C).astype(BF), "u": u.reshape(N, 128, 512).astype(BF), "v": v.astype(BF), **weights(rng, w.astype(BF))}
def setup_inputs_blocks(rng):
    d = numbers_of(rng)
    k = np.exp2(rng.integers(14, 19, (N, 8, 2, 1, C, 1)).astype(np.float64))
    s = (N, 8, 2, 8, C, 4)
    a = k * np.exp2(-rng.integers(8, 15, s).astype(np.float64)) * (1 + (2 * rng.integers(0, 64, s) + 1) * 2.0 ** -7) * rng.choice([-1.0, 1.0], s)
    a[:, :, :, 0, :, 0] = 1.96875 * k[:, :, :, 0, :, 0] * rng.choice([-1.0, 1.0], (N, 8, 2, C))
    u = d["u"].reshape(N, 128, 128, 4)
    e = rng.integers(N)
    for i in range(4): u[e, :, i::16] = 0
    w = layers(rng)
    w[:, :, ::8] = 0
    return {"x": a.astype(np.float32).reshape(N, 128, 4 * C).astype(BF), "u": u.reshape(N, 128, 512), "v": d["v"], **weights(rng, w)}
def setup_inputs_spread(rng):
    d = setup_inputs(rng)
    d["x"] = big(np.clip(wide(rng, N, 128, 4 * C, cols=6).astype(np.float32), -2.0 ** 21, 2.0 ** 21))
    return d
def check_inputs(d):
    b = []
    for k, top in (("x", 2.0 ** 21), ("u", 2.0 ** 30), ("v", 2.0 ** 30)):
        a = np.abs(d[k].astype(np.float32))
        if not (np.isfinite(a).all() and ((a == 0) | (a >= 2.0 ** -30) & (a <= top)).all()): b.append("a value of " + k)
    none, least, most = [emit(mx_ref.quantize(np.full((128, 16), k, np.float32).astype(BF)))[1][0, 0] for k in (0.0, 2.0 ** -30, 1.0)]
    for r in range(N):
        if ((d["wc"][r] == 0x7F) | (d["wc"][r] == 0xFF)).any(): b.append("wc: a code that is no number")
        s = mx_ref.live(d["ws"][r])
        if ((s != none) & ((s < least) | (s > most))).any(): b.append("ws: a scale out of range")
        elif (np.abs(decode(pk(d["wc"][r], d["ws"][r]))) > 1).any(): b.append("a number of W beyond 1")
    return b
def sources(s):
    order = np.argsort(-(s[::16] + np.float32(0.0)), axis=1, kind="stable")
    place = np.argsort(order, axis=1, kind="stable")
    kind = 1 * (s[1::16] > 0) + 2 * (s[2::16] > 0) + 4 * (s[3::16] > 0)
    used, j = np.zeros((C, 8), bool), np.arange(C)
    c = np.zeros((8, C), np.int64)
    for g in range(8):
        look = order[g][(place[(g + 1) % 8][:, None] + np.arange(A)) % C]
        new = ~used[j[:, None], kind[g][look]]
        c[g] = look[j, np.argmax(new, axis=1)]
        used[j, kind[g][c[g]]] = True
    return c
def reference(x, u, v, wc, ws):
    qu = [mx_ref.quantize(u[r]) for r in range(N)]
    lay = [[pick(pk(wc[r], ws[r]), np.arange(128 * b, 128 * b + 128)) for b in range(4)] for r in range(N)]
    now = [x[r] for r in range(N)]
    for h in STEP:
        q = [mx_ref.quantize(now[r]) for r in range(N)]
        own = [decode(q[r]) for r in range(N)]
        took = [sources(mx_ref.matmul(qu[r], q[r])) for r in range(N)]
        z = [mx_ref.quantize(gcols(own[r].astype(BF), took[r])) for r in range(N)]
        made = []
        for r in range(N):
            e = r ^ h
            back = mx_ref.quantize(tile([mx_ref.matmul(lay[e][b], z[r]) * np.float32(0.03125) + own[e][:, b::4] for b in range(4)]))
            first = np.full((8, C), -1)
            for g in range(8):
                for j in range(C - 1, -1, -1): first[g, took[r][g, j]] = j
            made.append((own[r] + gcols(decode(back).astype(BF), first).astype(np.float32)).astype(BF))
        now = made
    y, src = np.zeros((N, 128, C), np.float32), np.zeros((N, 8, C), np.float32)
    oc, osc = np.zeros((N, 128, 4 * C), np.uint8), np.zeros((N, 16, C), np.uint8)
    for r in range(N):
        p = mx_ref.quantize(now[r])
        y[r] = mx_ref.matmul(mx_ref.quantize(v[r]), p)
        src[r] = took[r]
        oc[r], osc[r] = emit(p)
    return {"y": y, "src": src, "oc": oc, "osc": osc}

import math
from concourse.mybir import dt, AluOpType, AxisListType, ActivationFunctionType

ROUNDS = [2, 1]
C = 256
_S = {}
AT = {}


def _b(names, n, d):
    for k in names.split():
        _S[k] = ("sbuf", [128, n], d)


def _parts(buf, d, names):
    o = 0
    for k, n in names:
        for m in k.split():
            AT[m] = (buf, o)
            o += n
    _b(buf, o, d)


F32, BF, I32, U16, Q8, S8 = "float32", "bfloat16", "int32", "uint16", "float8_e4m3fn_x4", "uint8"
_b("xt xn zt yt ff fp gt", 1024, BF)
_b("ut vin vt na fa z0 c32", 512, BF)
_b("dy", 1088, BF)
_b("cmp eq", 4096, BF)
_b("plb et", 2048, BF)
_b("ca", 2560, BF)
_b("c3", 1696, BF)
_b("wmask ea eb", 256, BF)
_b("tri onb", 128, BF)
_b("nn", 272, BF)
_b("srep", 2048, F32)
_b("yy kio wm1 wc1 wm2 wc2 cm cs crow yo k16 sctl", 256, F32)
_b("ord_ en one", 272, F32)
_b("osi osk", 272, I32)
_b("cu0 cu1 lz0 lz1", 16, U16)
_parts("small", F32, [("new uu ww", 128), ("tt", 144), ("ln la lb lc", 64), ("scol d1 d2 del_ nu x2f mm fm nf xzf ptr ptg pt m8", 16), ("m16", 32)])
_parts("csmall", F32, [("nrow mdiv bt0 bt1 bt2 ka0 ka1 ka2 pw pwi pwj", 128), ("qoff half zer", 64), ("pc", 16)])
_parts("ismall", I32, [("li", 64), ("fi hi lo", 16)])
_parts("cismall", I32, [("uli", 64), ("pint", 16), ("nli", 16)])
_parts("usmall", U16, [("x1u x2u xzu fku", 16)])
_parts("cusmall", U16, [("ulu", 64), ("nlu", 16)])
for _q, _n in [("wq", 512), ("qu", 128), ("qv", 128), ("ub", 1024), ("qx0", C), ("qx1", C), ("qx2", C), ("lx0", C), ("lx1", C), ("qz", C), ("qy0", C), ("qy1", C),
               ("ly0", C), ("ly1", C), ("qc", 1024), ("qe", 1024), ("qg", C), ("qt", 128), ("qn", 128), ("qf", 128), ("qE", 512), ("qa", 640), ("q3", 424)]:
    _S[_q] = ("sbuf", [128, _n], Q8)
    _S[_q + "s"] = ("sbuf", [128, _n], S8)
for _i in range(8):
    _S["b%d" % _i] = ("psum", [128, 512], F32)
SCRATCH = _S
SEMAPHORES = ["sv", "sa", "sp", "sg", "dx", "du", "dw", "dv", "dout", "loc", "ax0", "ax1", "az0", "az1", "ay0", "ay1"]

Op, Act = AluOpType, ActivationFunctionType
SEM = {"V": "sv", "S": "sa", "P": "sp", "G": "sg"}
PT0, MW, MV, KM, WQ = 0, 16, 32, 160, 294
CA20, ON = 256, 384


def rank_program(g, core, T, topo):
    rank = T.rank_of(core)
    if rank is None:
        return
    eng = {"V": g.vector, "S": g.scalar, "P": g.tensor, "G": g, "Y": g.sync}
    cnt = {}
    seen = {q: {} for q in eng}
    clock, recs = {}, {}

    def R(name, lo, hi, step=1):
        buf, o = AT.get(name, (name, 0))
        return (buf, o + lo, o + hi, step)

    def ap(r):
        return T[r[0]][:, r[1]:r[2]] if r[3] == 1 else T[r[0]][:, r[1]:r[2]:r[3]]

    def psum(r):
        return SCRATCH[r[0]][0] == "psum"

    def meets(a, b):
        if psum(a):
            return True
        return max(a[1], b[1]) < min(a[2], b[2]) and (a[1] - b[1]) % math.gcd(a[3], b[3]) == 0

    def covers(a, b):
        return psum(a) or (a[1] <= b[1] and a[2] >= b[2] and (a[3] == 1 or (a[3] == b[3] and (a[1] - b[1]) % a[3] == 0)))

    def order(q, reads, writes, acc):
        want = {}
        for r, w in [(r, False) for r in reads] + [(r, True) for r in writes]:
            for (o, ow, oq, (s, v)) in recs.get(r[0], []):
                if not meets(r, o):
                    continue
                hit = (w and not acc) or ow or (psum(r) and oq != q)
                if acc and w and oq == q:
                    hit = False
                if hit and seen[q].get(s, 0) < v:
                    want[s] = max(want.get(s, 0), v)
        for s in list(want):
            for s2 in want:
                if s2 != s and clock.get((s2, want[s2]), {}).get(s, 0) >= want[s] and not clock.get((s, want[s]), {}).get(s2, 0) >= want[s2]:
                    want[s] = 0
        for s, v in want.items():
            if v:
                eng[q].wait_ge(T.sem[s], v)
        for s, v in want.items():
            if v:
                for s2, v2 in list(clock.get((s, v), {}).items()) + [(s, v)]:
                    seen[q][s2] = max(seen[q].get(s2, 0), v2)

    def note(q, reads, writes, ev):
        clock[ev] = dict(seen[q])
        for r in writes:
            recs[r[0]] = [o for o in recs.get(r[0], []) if not covers(r, o[0])] + [(r, True, q, ev)]
        for r in reads:
            recs[r[0]] = [o for o in recs.get(r[0], []) if o[1] or o[2] != q or not covers(r, o[0])] + [(r, False, q, ev)]

    def do(q, fn, reads, writes, acc=False):
        order(q, reads, writes, acc)
        s = SEM[q]
        fn().then_inc(T.sem[s], 1)
        cnt[s] = cnt.get(s, 0) + 1
        note(q, reads, writes, (s, cnt[s]))

    def dma(q, out, in_, sem, reads=()):
        order(q, reads, [], False)
        eng[q].dma_start(out, in_).then_inc(T.sem[sem], 16)
        cnt[sem] = cnt.get(sem, 0) + 16

    def send(dst, pieces, sem):
        rid, pid, _ = topo.addr(dst)
        for out, in_, r in pieces:
            order("G", [r], [], False)
            g.remote_dma(out, in_, T.sem[sem], T.sem.loc, pid, rid, topo.mask(core, dst))
            cnt["loc"] = cnt.get("loc", 0) + len(topo.engines(core, dst))

    def arrives(src, sem, bufs):
        for r in bufs:
            recs.setdefault(r[0], []).append((r, True, "-", (sem, len(topo.engines(src, core)) * len(bufs))))

    def is_r(s):
        return isinstance(s, tuple)

    def sc(s):
        return ap(s) if is_r(s) else s

    def ms(out, val):
        do("V", lambda: g.vector.memset(ap(out), val), [], [out])

    def ts(out, in0, s1, s2, op0, op1=None):
        rd = [in0] + [s for s in (s1, s2) if is_r(s)]
        if op1 is None:
            do("V", lambda: g.vector.tensor_scalar(ap(out), ap(in0), sc(s1), None, op0), rd, [out])
        else:
            do("V", lambda: g.vector.tensor_scalar(ap(out), ap(in0), sc(s1), sc(s2), op0, op1), rd, [out])

    def tt(out, in0, in1, op, off=None):
        if off is None:
            do("V", lambda: g.vector.tensor_tensor(ap(out), ap(in0), ap(in1), op), [in0, in1], [out])
        else:
            do("V", lambda: g.vector.tensor_tensor(ap(out), ap(in0).indirect(ap(off)), ap(in1), op), [in0, in1, off], [out])

    def cp(out, in_, off=None):
        if off is None:
            do("V", lambda: g.vector.tensor_copy(ap(out), ap(in_)), [in_], [out])
        else:
            do("V", lambda: g.vector.tensor_copy(ap(out), ap(in_).indirect(ap(off))), [in_, off], [out])

    def scan(out, d0, d1, init, op0, op1):
        do("V", lambda: g.vector.tensor_tensor_scan(ap(out), ap(d0), ap(d1), init, op0, op1), [d0, d1], [out])

    def least(out, in_):
        do("V", lambda: g.vector.tensor_reduce(ap(out), ap(in_), AxisListType.X, Op.min), [in_], [out])

    def act(out, in_, func, bias=0.0, scale=1.0, off=None):
        rd = [in_] + [s for s in (bias, scale, off) if is_r(s)]
        i = ap(in_) if off is None else ap(in_).indirect(ap(off))
        do("S", lambda: g.scalar.activation(ap(out), i, func, bias=sc(bias), scale=sc(scale)), rd, [out])

    def mx(bank, n, lhs, lo, rhs, ro, start=True, stop=True):
        rd = [R(lhs, lo, lo + 128), R(lhs + "s", lo, lo + 128), R(rhs, ro, ro + n), R(rhs + "s", ro, ro + n)]
        out = R(bank, 0, n)
        do("P", lambda: g.tensor.matmul_mx(ap(out), ap(rd[0]), ap(rd[1]), ap(rd[2]), ap(rd[3]), start, stop), rd, [out], not start)

    def quant(q, lo, n, in_):
        c, s = R(q, lo, lo + n), R(q + "s", lo, lo + n)
        do("V", lambda: g.vector.quantize_mx(ap(c), ap(s), ap(in_)), [in_], [c, s])

    def iota(out, pattern, base=0, cm=0):
        do("G", lambda: g.iota(ap(out), pattern, base, cm, allow_small_or_imprecise_dtypes=True), [], [out])

    def select(out, in_, pattern, cmp, base, cm):
        do("G", lambda: g.affine_select(ap(out), ap(in_), pattern, cmp, 0.0, base, cm), [in_], [out])

    for q, name, src, sem in (("Y", "xt", T.x, "dx"), ("S", "ut", T.u, "du"), ("Y", "wq", T.wc, "dw"), ("Y", "wqs", T.ws, "dw"), ("Y", "vin", T.v, "dv")):
        w = SCRATCH[name][1][1]
        dma(q, T[name][:, 0:w].bitcast(dt.uint8) if name == "wq" else T[name][:, 0:w], src[:, :], sem)
        recs[name] = [(R(name, 0, w), True, "-", (sem, 32 if sem == "dw" else 16))]

    def fill(out, val):
        act(out, R("z0", 0, (out[2] - out[1] + out[3] - 1) // out[3]), Act.Identity, bias=val)

    def ones(put, buf, w0, w1, e):
        for t in (2 * e, 2 * e + 1):
            put(R(buf, 4 * w0 + t, 4 * w1, 4), 1.0)

    ms(R("z0", 0, 512), 0.0)
    ms(R("onb", 0, 128), 1.0)
    ms(R("c32", 0, 512), 32.0)
    ms(R("ca", 0, 1536), 0.0)
    iota(R("uli", 0, 64), [[16, 8], [0, 8]])
    iota(R("pint", 0, 1), [[0, 1]], 0, 1)
    for i in range(3):
        iota(R("bt%d" % i, 0, 128), [[0, 64 >> i], [1, 2], [0, 1 << i]])
    iota(R("nrow", 0, 128), [[1, 128]])
    iota(R("mdiv", 0, 128), [[1, 8], [0, 16]])
    iota(R("k16", 0, 256), [[0, 16], [1, 16]])
    select(R("tri", 0, 128), R("onb", 0, 128), [[1, 128]], Op.is_gt, 0, -1)
    for k in range(4):
        fill(R("c3", 424 * k, 424 * k + 424), 0.0)
    for k in range(2):
        fill(R("gt", 512 * k, 512 * k + 512), 0.0)
    cp(R("ulu", 0, 64), R("uli", 0, 64))
    ones(ms, "ca", 128, 144, 0)
    ones(ms, "ca", 144, 160, 1)
    ones(ms, "ca", CA20, CA20 + 16, 1)
    ones(ms, "ca", CA20 + 112, CA20 + 128, 0)
    quant("qa", 0, 384, R("ca", 0, 1536))
    ts(R("pint", 1, 2), R("pint", 0, 1), 15, None, Op.bitwise_and)
    ts(R("pint", 2, 3), R("pint", 0, 1), 4, None, Op.arith_shift_right)
    ts(R("pint", 3, 4), R("pint", 0, 1), 8, None, Op.bitwise_and)
    cp(R("pc", 0, 4), R("pint", 0, 4))

    def picks(p):
        o, k = R("ub", 256 * p, 256 * p + 256), R("ulu", 16 * p, 16 * p + 16)
        os_ = R("ubs", 256 * p, 256 * p + 256)
        do("V", lambda: g.vector.tensor_copy(ap(o).bitcast(dt.uint32), T.qu[:, 0:128].bitcast(dt.uint32).indirect(ap(k))), [R("qu", 0, 128), k], [o])
        do("S", lambda: g.scalar.activation(ap(os_), T.qus[:, 0:128].indirect(ap(k)), Act.Copy), [R("qus", 0, 128), k], [os_])

    quant("qu", 0, 128, R("ut", 0, 512))
    picks(0)
    quant("qx0", 0, 256, R("xt", 0, 1024))
    picks(1)

    def class_constants():
        for i in range(3):
            ts(R("pc", 4 + i, 5 + i), R("pc", 1, 2), float(i + 1), -512.0, Op.is_equal, Op.mult)
            ts(R("pc", 7 + i, 8 + i), R("pc", 1, 2), float(i + 1), 256.0, Op.is_equal, Op.mult)
        for i in range(3):
            act(R("ka%d" % i, 0, 128), R("bt%d" % i, 0, 128), Act.Identity, bias=R("pc", 7 + i, 8 + i), scale=R("pc", 4 + i, 5 + i))
        ones(fill, "c3", PT0 + 6, PT0 + 7, 0)
        ones(fill, "c3", PT0 + 7, PT0 + 8, 1)
        ones(fill, "c3", PT0 + 14, PT0 + 15, 0)

    def more_constants():
        tt(R("pc", 10, 11), R("pc", 0, 1), R("pc", 1, 2), Op.add)
        ts(R("pc", 11, 12), R("pc", 3, 4), 100.0, None, Op.mult)
        tt(R("ka0", 0, 128), R("ka0", 0, 128), R("ka1", 0, 128), Op.add)
        ts(R("mdiv", 0, 128), R("mdiv", 0, 128), R("pc", 2, 3), None, Op.is_equal)
        tt(R("pc", 12, 13), R("pc", 11, 12), R("pc", 10, 11), Op.add)
        ts(R("pc", 14, 15), R("pc", 2, 3), 8.0, None, Op.add)
        tt(R("ka0", 0, 128), R("ka0", 0, 128), R("ka2", 0, 128), Op.add)
        ts(R("pc", 13, 14), R("pc", 12, 13), 1.0, None, Op.add)
        ts(R("wmask", 0, 256), R("k16", 0, 256), R("pc", 1, 2), None, Op.is_equal)
        tt(R("c3", 4 * KM, 4 * KM + 512, 4), R("ka0", 0, 128), R("mdiv", 0, 128), Op.mult)
        for e in range(2):
            ts(R("c3", 4 * MV + e, 4 * MV + 512, 4), R("nrow", 0, 128), R("pc", 12 + e, 13 + e), None, Op.is_equal)
            for nib in range(2):
                ts(R("c3", 4 * MW + e + 2 * nib, 4 * MW + 64, 4), R("nrow", 0, 16), R("pc", 2, 3) if e == 0 else R("pc", 14, 15), float(16 ** nib), Op.is_equal, Op.mult)
        quant("q3", 0, 288, R("c3", 0, 1152))

    def later_constants():
        iota(R("kio", 0, 256), [[1, 256]], 768)
        iota(R("nli", 0, 8), [[1, 8]])
        iota(R("qoff", 0, 64), [[0, 2], [64, 4], [0, 8]])
        for b in range(4):
            select(R("et", 512 * b, 512 * b + 512), R("c32", 0, 512), [[-1, 512]], Op.is_equal, b, 4)
        fill(R("one", 0, 272), 1.0)
        fill(R("sctl", 0, 256), 1.0)
        fill(R("sctl", 0, 256, 16), 0.0)
        fill(R("tt", 0, 144), 11.5)
        fill(R("half", 0, 64), 0.5)
        fill(R("zer", 0, 64), 0.0)
        for k in range(2):
            fill(R("ca", 4 * ON + 512 * k, 4 * ON + 512 * k + 512), 0.0)
            ones(fill, "ca", ON + 128 * k, ON + 128 * k + 128, k)
        for i in range(2):
            scan(R("pw", 64 * i, 64 * i + 64), R("half", 0, 64), R("zer", 0, 64), 2.0 ** 31, Op.mult, Op.add)
        select(R("pwi", 0, 128), R("pw", 0, 128), [[-1, 128]], Op.is_equal, 0, 1)
        wc = R("pc", 15, 16)
        do("S", lambda: g.scalar.activation(ap(R("pwj", 0, 128)), ap(R("pwi", 0, 128)), Act.Copy, accum_out=ap(wc)), [R("pwi", 0, 128)], [R("pwj", 0, 128), wc])
        for k in range(4):
            for e in range(2):
                col, p = 4 * (WQ + 8 * k + e) + 2 * e + k // 2, 64 * (k % 2)
                do("S", lambda: g.scalar.activation(T.c3[p:p + 64, col:col + 1], T[wc[0]][p:p + 64, wc[1]:wc[2]], Act.Copy), [wc], [R("c3", col, col + 1)])
        for nm in ("vt", "na", "fa"):
            fill(R(nm, 0, 512), 0.0)
        for b in range(4):
            fill(R("dy", 272 * b + 256, 272 * b + 272), 0.0)
        cp(R("nlu", 0, 8), R("nli", 0, 8))
        quant("qE", 0, 512, R("et", 0, 2048))
        quant("qa", ON, 256, R("ca", 4 * ON, 2560))

    ulp, tiny = 2.0 ** -24 * (1 + 2.0 ** -22), 2.0 ** -120

    def one_round(rd):
        mate = T.cores[rank ^ ROUNDS[rd]]
        qx, lx, qy, ly = "qx%d" % rd, "lx%d" % rd, "qy%d" % rd, "ly%d" % rd
        cu, lz = "cu%d" % rd, "lz%d" % rd

        def codes(q):
            return T[q][:, 0:C].bitcast(dt.uint8)

        def share(a, b, sem):
            send(mate, [(codes(b), codes(a), R(a, 0, C)), (T[b + "s"][:, 0:C], T[a + "s"][:, 0:C], R(a + "s", 0, C))], sem)
            arrives(mate, sem, [R(b, 0, C), R(b + "s", 0, C)])

        share(qx, lx, "ax%d" % rd)
        mx("b0", 128, qx, 0, "qu", 0)
        mx("b1", 128, qx, 128, "qu", 0)
        mx("b2", 256, "qu", 0, qx, 0)
        bank = ["b3", "b4", "b5"]
        for k in range(3):
            mx(bank[k], 256, "ub", 128 * k, qx, 0)
        for h in range(2):
            cp(R("scol", 8 * h, 8 * h + 8), R("b%d" % h, 0, 128, 16))
        ts(R("d1", 0, 16), R("scol", 0, 16), ulp, tiny, Op.mult, Op.max)
        ts(R("d2", 0, 16), R("scol", 0, 16), -ulp, None, Op.mult)
        tt(R("del_", 0, 16), R("d1", 0, 16), R("d2", 0, 16), Op.max)
        tt(R("nu", 0, 16), R("scol", 0, 16), R("del_", 0, 16), Op.add)
        for k in range(8):
            for h in range(2):
                c = 8 * h + k
                act(R("srep", 256 * k + 128 * h, 256 * k + 128 * h + 128), R("tri", 0, 128), Act.Identity, bias=R("scol", c, c + 1), scale=R("del_", c, c + 1))
            if k == 3:
                if rd == 0:
                    class_constants()
                act(R("gt", 0, 1024, 4), R("b2", 0, 256), Act.Sign, bias=-2.0 ** -110)
        for k in range(8):
            p, e, bk = k // 2, k % 2, bank[k % 3]
            for h in range(2):
                t = 1024 * p + 2 * e + h
                o = 128 * (1 - h)
                ts(R("cmp", t + 4 * o, t + 4 * o + 509, 4), R(bk, o, o + 128), R("nu" if h == 0 else "scol", 8 * h + k, 8 * h + k + 1), None, Op.is_lt)
            for h in range(2):
                t = 1024 * p + 2 * e + h
                o = 128 * h
                tt(R("cmp", t + 4 * o, t + 4 * o + 509, 4), R(bk, o, o + 128), R("srep", 256 * k + o, 256 * k + o + 128), Op.is_lt)
            if k + 3 < 8:
                if rd == 0 and k in (0, 2):
                    picks(2 + k // 2)
                mx(bank[k % 3], 256, "ub", 128 * (k + 3), qx, 0)
            if e:
                quant("qc", 256 * p, 256, R("cmp", 1024 * p, 1024 * p + 1024))
                mx("b6", 256, "qa", 128 - 32 * p, "qc", 256 * p, p == 0, p == 3)
                mx("b7", 256, "qa", 144 - 32 * p if p else CA20, "qc", 256 * p, p == 0, p == 3)
                if rd == 0 and p == 1:
                    more_constants()
                if p == 2:
                    quant("qg", 0, 256, R("gt", 0, 1024))
                    mx("b2", 256, "q3", KM, "qg", 0)
        if rd == 0:
            later_constants()

        def wrap(bk, a, b):
            tt(R(a, 0, 256), R(bk, 0, 256), R("wmask", 0, 256), Op.mult)
            scan(R(b, 0, 256), R("sctl", 0, 256), R(a, 0, 256), 0.0, Op.mult, Op.add)

        for q, f, banks in ((qx, "ff", ("b3", "b4", "b5", "b0")), (lx, "fp", ("b1", "b3", "b4", "b5"))):
            for b in range(4):
                mx(banks[b], 256, "qE", 128 * b, q, 0)
                act(R(f, 256 * b, 256 * b + 256), R(banks[b], 0, 256), Act.Copy, scale=0.03125)
        tt(R("yy", 0, 256), R("b2", 0, 256), R("kio", 0, 256), Op.add)
        wrap("b6", "wm1", "wc1")
        ts(R("x1u", 0, 16), R("wc1", 15, 256, 16), -1.0, 266.0, Op.mult, Op.add)
        o267, y256, x16 = R("ord_", 0, 267), R("yy", 0, 256), R("x1u", 0, 16)
        do("V", lambda: g.vector.tensor_copy(ap(o267).indirect(ap(x16)), ap(y256)), [y256, x16], [o267])
        wrap("b7", "wm2", "wc2")
        cp(R("ord_", 0, 11), R("ord_", 256, 267))
        ts(R("x2u", 0, 16), R("wc2", 15, 256, 16), -1.0, 266.0, Op.mult, Op.add)
        ts(R("en", 0, 267), R("ord_", 0, 267), 512.0, 16.0, Op.is_ge, Op.mult)
        ts(R("x2f", 0, 16), R("wc2", 15, 256, 16), -1.0, 266.0, Op.mult, Op.add)
        scan(R("nn", 0, 267), R("one", 0, 267), R("en", 0, 267), 16.0, Op.add, Op.min)
        for e in range(2):
            cp(R("vt", e, 512, 4), R("nn", 0, 267), R("x2u", 8 * e, 8 * e + 8))
        quant("qt", 0, 128, R("vt", 0, 512))
        mx("b2", 128, "qt", 0, "q3", MV)
        cp(R("osi", 0, 267), R("ord_", 0, 267))
        ts(R("osk", 0, 267), R("osi", 0, 267), 511, None, Op.bitwise_and)
        for h in range(2):
            for p in range(4):
                mx("b%d" % (6 + h), 128, "qc", 256 * p + 128 * h, "q3", PT0 + 6 - 2 * p, p == 0, p == 3)
        for k in range(8):
            bk = ("b0", "b1", "b3", "b4")[k % 4]
            mx(bk, 256, "qa", ON + 128 * (k % 2), "qc", 256 * (k // 2))
            act(R("plb", 256 * k, 256 * k + 256), R(bk, 0, 256), Act.Copy)

        def V(k):
            return R("b2", 16 * k, 16 * k + 16)

        def blk(nm, k):
            return R(nm, 16 * k, 16 * k + 16)

        cp(R("tt", 0, 16), V(0))
        for k in range(8):
            o = 18 * k
            for e in range(2):
                least(R("mm", 8 * e + k, 8 * e + k + 1), R("tt", o + e, o + 18, 2))
            if k < 7:
                used = blk("new", 0) if k == 1 else blk("uu", k)
                if k:
                    tt(blk("ww", k + 1), V(k + 1), used, Op.add)
                for e in range(2):
                    ts(R("new", 16 * k + e, 16 * k + 16, 2), R("tt", o + e, o + 16, 2), R("mm", 8 * e + k, 8 * e + k + 1), 64.0, Op.is_equal, Op.mult)
                tt(R("tt", o + 18, o + 34), V(1) if k == 0 else blk("ww", k + 1), blk("new", k), Op.add)
                if 1 <= k < 6:
                    tt(blk("uu", k + 1), used, blk("new", k), Op.add)
        ts(R("fm", 0, 16), R("mm", 0, 16), 11.25, None, Op.is_lt)
        tt(R("nf", 0, 16), R("mm", 0, 16), R("fm", 0, 16), Op.mult)
        for e in range(2):
            tt(R("na", e, 512, 4), R("nf", 8 * e, 8 * e + 8), R("wmask", 0, 128), Op.mult, R("nlu", 0, 8))
        quant("qn", 0, 128, R("na", 0, 512))
        mx("b5", 128, "qn", 0, "q3", MW)
        ybank = ("b3", "b4", "b0", "b1")
        for b in range(4):
            mx(ybank[b], 256, "qE", 128 * b, qx, 0, True, False)
        for h in range(2):
            tt(R("ptr", 8 * h, 8 * h + 8), R("b%d" % (6 + h), 1, 9), R("nf", 8 * h, 8 * h + 8), Op.add)
        tt(R("xzf", 0, 16), R("x2f", 0, 16), R("b5", 0, 16), Op.subtract)
        cp(R("xzu", 0, 16), R("xzf", 0, 16))
        tt(R("cm", 0, 256), R("osk", 0, 267), R("wmask", 0, 256), Op.mult, R("xzu", 0, 16))
        scan(R("cs", 0, 256), R("sctl", 0, 256), R("cm", 0, 256), 0.0, Op.mult, Op.add)
        cp(R(cu, 0, 16), R("cs", 15, 256, 16))
        send(mate, [(T[lz][:, 0:16], T[cu][:, 0:16], R(cu, 0, 16))], "az%d" % rd)
        arrives(mate, "az%d" % rd, [R(lz, 0, 16)])

        ts(R("ptg", 0, 16), R("ptr", 0, 16), 256.0, -256.0, Op.is_ge, Op.mult)
        tt(R("pt", 0, 16), R("ptr", 0, 16), R("ptg", 0, 16), Op.add)
        for k in range(8):
            for h in range(2):
                t = 1024 * (k // 2) + 2 * (k % 2) + h
                eq, row, col = R("eq", t, t + 1021, 4), R("plb", 256 * k, 256 * k + 256), R("pt", 8 * h + k, 8 * h + k + 1)
                if k < 6:
                    ts(eq, row, col, None, Op.is_equal)
                else:
                    tmp = R("ea" if h == 0 else "eb", 0, 256)
                    act(tmp, row, Act.Abs, bias=col, scale=-1.0)
                    act(eq, tmp, Act.Relu, bias=1.0, scale=-1.0)
        if rd == 0:
            quant("q3", 288, 136, R("c3", 1152, 1696))
            quant("qv", 0, 128, R("vin", 0, 512))
        for b in range(4):
            o, w = R("zt", b, 1024, 4), R("fp", 256 * b, 256 * b + 256)
            if b % 2 == 0:
                cp(o, w, R(lz, 0, 16))
            else:
                act(o, w, Act.Copy, off=R(lz, 0, 16))
        quant("qz", 0, 256, R("zt", 0, 1024))
        for b in range(4):
            mx(ybank[b], 256, "wq", 128 * b, "qz", 0, False, True)
        for p in range(4):
            quant("qe", 256 * p, 256, R("eq", 1024 * p, 1024 * p + 1024))
        for b in range(4):
            o, w = R("yt", b, 1024, 4), R(ybank[b], 0, 256)
            if b == 3:
                ts(o, w, 0.03125, None, Op.mult)
            else:
                act(o, w, Act.Copy, scale=0.03125)
        quant(qy, 0, 256, R("yt", 0, 1024))
        share(qy, ly, "ay%d" % rd)
        for h in range(2):
            for p in range(4):
                mx("b%d" % (6 + h), 128, "qe", 256 * p + 128 * h, "q3", WQ - 2 * p, p == 0, p == 3)
            act(R("ln", 32 * h, 32 * h + 32), R("b%d" % (6 + h), 0, 32), Act.Ln, bias=2.0 ** -50)
        ts(R("la", 0, 64), R("ln", 0, 64), -1.0 / math.log(2.0), 30.49982, Op.mult, Op.add)
        cp(R("li", 0, 64), R("la", 0, 64))
        ts(R("lb", 0, 64), R("li", 0, 64), 64.0, 512.0, Op.is_ge, Op.mult)
        tt(R("lc", 0, 64), R("li", 0, 64), R("qoff", 0, 64), Op.add)
        tt(R("lb", 0, 64), R("lb", 0, 64), R("lc", 0, 64), Op.add)
        for h in range(2):
            tt(R("m16", 16 * h, 16 * h + 16), R("lb", 32 * h, 32 * h + 16), R("lb", 32 * h + 16, 32 * h + 32), Op.min)
        for h in range(2):
            tt(R("m8", 8 * h, 8 * h + 8), R("m16", 16 * h, 16 * h + 8), R("m16", 16 * h + 8, 16 * h + 16), Op.min)
        ts(R("fi", 0, 16), R("m8", 0, 16), 256.0, None, Op.min)
        ts(R("lo", 0, 16), R("fi", 0, 16), 15, None, Op.bitwise_and)
        ts(R("hi", 0, 16), R("fi", 0, 16), 4, None, Op.arith_shift_right)
        for nib, nm in enumerate(("lo", "hi")):
            for h in range(2):
                tt(R("fa", h + 2 * nib, 512, 4), R(nm, 8 * h, 8 * h + 8), R("wmask", 0, 128), Op.mult, R("nlu", 0, 8))
        quant("qf", 0, 128, R("fa", 0, 512))
        mx("b2", 128, "qf", 0, "q3", MW)
        cp(R("fku", 0, 16), R("b2", 0, 16))
        if rd == 1:
            cp(R("crow", 0, 256), R("osk", 0, 267), R("xzu", 0, 16))
            dma("Y", T.src[:, :], T.crow[0:128:16, 0:256], "dout", [R("crow", 0, 256)])
        for b in range(4):
            mx(ybank[b], 256, "qE", 128 * b, ly, 0)
            act(R("dy", 272 * b, 272 * b + 256), R(ybank[b], 0, 256), Act.Copy, scale=0.03125)
        for b in range(4):
            tt(R("xn", b, 1024, 4), R("dy", 272 * b, 272 * b + 272), R("ff", 256 * b, 256 * b + 256), Op.add, R("fku", 0, 16))
        quant("qx%d" % (rd + 1), 0, 256, R("xn", 0, 1024))

    for rd in range(2):
        one_round(rd)
    mx("b0", 256, "qv", 0, "qx2", 0)
    dma("Y", T.oc[:, 0:4 * C], T.qx2[:, 0:C].bitcast(dt.uint8), "dout", [R("qx2", 0, C)])
    for k in range(4):
        dma("S", T.osc[4 * k:4 * k + 4, 0:C], T.qx2s[32 * k:32 * k + 4, 0:C], "dout", [R("qx2s", 0, C)])
    cp(R("yo", 0, C), R("b0", 0, C))
    dma("Y", T.y[:, :], T.yo[:, 0:C], "dout", [R("yo", 0, C)])
    for s in ("sv", "sa", "sp", "sg", "loc", "dout"):
        g.wait_ge(T.sem[s], cnt[s])
